import numpy as np
import ml_dtypes


def mxq(x, axis, fmt="e4m3"):
    dtype, down = {"e4m3": (ml_dtypes.float8_e4m3fn, 7), "e5m2": (ml_dtypes.float8_e5m2, 14)}[fmt]
    v = np.moveaxis(np.asarray(x, np.float32).astype(ml_dtypes.bfloat16).astype(np.float64), axis, -1)
    blocks = v.reshape(v.shape[:-1] + (-1, 32))
    amax = np.abs(blocks).max(-1, keepdims=True)
    byte = np.maximum(np.where(amax > 0, np.frexp(amax)[1] - 1 + 127, 0) - down, 1)
    scale = np.exp2(byte - 127.0)
    codes = (blocks / scale).astype(np.float32).astype(dtype).astype(np.float64)
    return np.moveaxis((codes * scale).reshape(v.shape), -1, axis)


WIDE = False


def mx_kscale(k):
    if not WIDE:
        return np.ones(k)
    levels = np.array([10, -10, 5, -5, 0])
    if k % 512:
        return np.exp2(np.random.permutation(np.resize(levels, k // 32))).repeat(32)
    a = np.empty((k // 512, 16))
    for p in range(k // 512):
        a[p, :8] = np.random.permutation(np.resize(levels, 8))
        for g in range(8):
            far = levels[np.abs(levels - a[p, g]) >= 10]
            a[p, g + 8] = far[np.random.randint(len(far))]
    return np.exp2(a.ravel()).repeat(32)


def f64(x):
    return np.asarray(x).astype(np.float64)


def striped(idx):
    return np.tile(np.asarray(idx).reshape(-1, 16).T, (8, 1)).astype(np.uint16)


def unstriped(offs):
    return offs[:16].T.reshape(-1).astype(np.int64)


E2M1 = np.array([0.0, 0.5, 1.0, 1.5, 2.0, 3.0, 4.0, 6.0, -0.0, -0.5, -1.0, -1.5, -2.0, -3.0, -4.0, -6.0])


def pack_weight(w, fmt):
    k, n = w.shape
    w = f64(np.asarray(w, np.float32).astype(ml_dtypes.bfloat16)).reshape(k // 32, 32, n)
    amax = np.abs(w).max(1)
    if fmt == "e4m3":
        byte = np.frexp(amax)[1] - 1 + 127 - 7
    else:
        mant, ex = np.frexp(amax / 6.0)
        byte = np.where(mant > 0.5, ex, ex - 1) + 127
    byte = np.clip(np.where(amax > 0, byte, 1), 1, 254)
    scaled = (w * np.exp2(127.0 - byte)[:, None, :]).reshape(k, n).astype(np.float32)
    by_word = np.ascontiguousarray(scaled.reshape(k // 512, 128, 4, n).transpose(0, 1, 3, 2))
    if fmt == "e4m3":
        words = by_word.astype(ml_dtypes.float8_e4m3fn).view(np.uint8)
    else:
        c = by_word.astype(ml_dtypes.float4_e2m1fn).view(np.uint8) & 0xF
        words = (c[..., 0::2] | (c[..., 1::2] << 4)).reshape(k // 512, 128, 2 * n)
    return np.ascontiguousarray(words), np.ascontiguousarray(byte.astype(np.uint8).reshape(k // 512, 16, n))


def unpack_weight(words, scales, fmt):
    g, _, n = scales.shape
    words = np.ascontiguousarray(words).reshape(g, 128, n, -1)
    if fmt == "e4m3":
        vals = words.view(ml_dtypes.float8_e4m3fn).astype(np.float64)
    else:
        nib = np.empty((g, 128, n, 4), np.uint8)
        nib[..., 0::2] = words & 0xF
        nib[..., 1::2] = words >> 4
        vals = E2M1[nib]
    vals = vals * np.repeat(np.exp2(scales.astype(np.float64) - 127.0), 8, axis=1)[..., None]
    return vals.transpose(0, 1, 3, 2).reshape(g * 512, n)


def sigmoid(v):
    return 1.0 / (1.0 + np.exp(-v))


K, I, L, S, T, N, M = 1024, 512, 512, 512, 512, 512, 512


def setup_inputs():
    n = np.random.standard_normal
    idx = np.random.randint(0, I, T)
    idx2 = np.random.randint(0, S, T)
    fk = mx_kscale(K)
    fl = mx_kscale(L)
    fm = mx_kscale(M)
    xap = pack_weight(n((K, I)) / fk[:, None], "e4m3")
    xbp = pack_weight(n((L, S)) / fl[:, None], "e2m1")
    wbp = pack_weight(n((L, N)) * 1 / np.sqrt(L) * fl[:, None], "e4m3")
    xgp = pack_weight(n((M, T)) / fm[:, None], "e2m1")
    wgp = pack_weight(n((M, N)) * 1 / np.sqrt(M) * fm[:, None], "e4m3")
    return {
        "xa_words": xap[0],
        "xa_scales": xap[1],
        "wa": (n((K, N)) * 1 / np.sqrt(K) * fk[:, None]).astype(np.float32),
        "xb_words": xbp[0],
        "xb_scales": xbp[1],
        "wb_words": wbp[0],
        "wb_scales": wbp[1],
        "xg_words": xgp[0],
        "xg_scales": xgp[1],
        "wg_words": wgp[0],
        "wg_scales": wgp[1],
        "offs": striped(idx),
        "offs2": striped(idx2),
    }


def reference(xa_words, xa_scales, wa, xb_words, xb_scales, wb_words, wb_scales, xg_words, xg_scales, wg_words, wg_scales, offs, offs2):
    idx = unstriped(offs)
    idx2 = unstriped(offs2)
    xau = unpack_weight(xa_words, xa_scales, "e4m3")
    xbu = unpack_weight(xb_words, xb_scales, "e2m1")
    wbu = unpack_weight(wb_words, wb_scales, "e4m3")
    xgu = unpack_weight(xg_words, xg_scales, "e2m1")
    wgu = unpack_weight(wg_words, wg_scales, "e4m3")
    waq = mxq(f64(wa), 0, "e4m3")
    za = waq.T @ xau
    zb = wbu.T @ xbu
    g = wgu.T @ xgu
    y = zb[:, idx2] + sigmoid(g) * (za[:, idx] - zb[:, idx2])
    return y

@@ -1,0 +1,162 @@
+from contextlib import ExitStack
+
+import concourse.mybir as mybir
+
+K, SLOTS, T, N = 1024, 512, 512, 512
+FLOPS = 2 * N * (K * SLOTS + 512 * SLOTS + 512 * T)
+
+F32 = mybir.dt.float32
+BF16 = mybir.dt.bfloat16
+I32 = mybir.dt.int32
+U16 = mybir.dt.uint16
+U8 = mybir.dt.uint8
+FP8X4 = mybir.dt.float8_e4m3fn_x4
+FP4X4 = mybir.dt.float4_e2m1fn_x4
+SIGMOID = mybir.ActivationFunctionType.Sigmoid
+MULT = mybir.AluOpType.mult
+ADD = mybir.AluOpType.add
+
+P = 128
+PACK = 4
+PASSES = 2
+BLOCKS = N // P
+HALF = T // 2
+
+
+def tile_moe_combine_gated_by_token_kernel(
+    tc, xa_words, xa_scales, wa, xb_words, xb_scales, wb_words, wb_scales,
+    xg_words, xg_scales, wg_words, wg_scales, offs, offs2, out,
+):
+    nc = tc.nc
+    with ExitStack() as ctx:
+        held = ctx.enter_context(tc.tile_pool(name="held", bufs=1))
+        psum = ctx.enter_context(tc.psum_pool(name="psum", bufs=1))
+
+        def tile(name, shape, dtype):
+            return held.tile(shape, dtype, name=name, align_bytes=64)
+
+        late = ctx.enter_context(tc.tile_pool(name="late", bufs=1))
+        stage = late.tile([P, 6, 4, 128], I32, name="stage", offset=2048)
+        planes = tile("planes", [P, 6, 512], U8)
+        nc.vector.memset(planes[:].bitcast(I32), 0)
+        for j, scales in ((0, xb_scales), (1, wb_scales), (2, xg_scales), (3, wg_scales), (4, xa_scales)):
+            passes = scales.shape[0]
+            nc.sync.dma_start(
+                stage[0:4, j:j + passes].rearrange("r z q c -> r (z q) c"),
+                scales.rearrange("z (q r) c -> r (z q) c", r=4).bitcast(I32),
+            )
+
+        def load_wa(dst, h, z):
+            nc.sync.dma_start(dst[:], wa[512 * z:512 * (z + 1), 256 * h:256 * (h + 1)].rearrange("(p j) c -> p j c", j=PACK))
+
+        xb = tile("xb", [P, 2 * SLOTS], U8)
+        wb = tile("wb", [P, N], I32)
+        xg = tile("xg", [P, 2 * T], U8)
+        wg = tile("wg", [P, N], I32)
+        list_a = held.tile([P, T // 16], U16, name="list_a")
+        list_b = held.tile([P, T // 16], U16, name="list_b")
+        raw = {(0, 0): tile("raw00", [P, PACK, 256], F32)}
+        nc.sync.dma_start(xb[:].bitcast(I32), xb_words[0].bitcast(I32))
+        nc.sync.dma_start(wb[:], wb_words[0].rearrange("p n t -> p (n t)").bitcast(I32))
+        load_wa(raw[0, 0], 0, 0)
+        nc.sync.dma_start(wg[:], wg_words[0].rearrange("p n t -> p (n t)").bitcast(I32))
+        nc.sync.dma_start(xg[:].bitcast(I32), xg_words[0].bitcast(I32))
+        nc.sync.dma_start(list_b[:], offs2)
+        nc.sync.dma_start(list_a[:], offs)
+
+        words = planes[:].bitcast(I32)
+        nc.vector.tensor_copy(words[0:4], stage[0:4, :, 0])
+        for q in range(1, 4):
+            nc.scalar.dma_start(words[32 * q:32 * q + 4], stage[0:4, :, q])
+
+        raw[0, 1] = late.tile([P, PACK, 256], F32, name="raw01", offset=0)
+        load_wa(raw[0, 1], 0, 1)
+        xa = late.tile([P, PASSES, SLOTS], I32, name="xa", offset=4096, align_bytes=64)
+        nc.sync.dma_start(xa[:], xa_words.rearrange("z p c t -> p z (c t)").bitcast(I32))
+        for z in range(PASSES):
+            raw[1, z] = late.tile([P, PACK, 256], F32, name=f"raw1{z}", offset=4096 * (z + 2))
+            load_wa(raw[1, z], 1, z)
+
+        def gated(dst, table, lst, gate, h):
+            cols = slice(h * HALF, (h + 1) * HALF)
+            nc.vector.tensor_tensor(dst[:, cols], table[:].indirect(lst[:, h * 16:(h + 1) * 16]), gate[:, cols], MULT)
+
+        grouped = [tile(f"grouped{b}", [P, PASSES, P, PACK], BF16) for b in range(BLOCKS)]
+        codes = [tile(f"code{b}", [P, PASSES * P], I32) for b in range(BLOCKS)]
+        wa_planes = [tile(f"wa_plane{b}", [P, PASSES * P], U8) for b in range(BLOCKS)]
+
+        def interleave(b, z):
+            src = raw[b // 2, z][:, :, (b % 2) * P:(b % 2 + 1) * P].rearrange("p t (c i) -> p c t i", i=4)
+            dst = grouped[b][:, z].rearrange("p (c i) t -> p c t i", i=4)
+            if b < 2:
+                nc.vector.tensor_copy(dst, src)
+            else:
+                nc.scalar.copy(dst, src)
+
+        def quantize(b):
+            nc.vector.quantize_mx(codes[b][:].bitcast(FP8X4), wa_planes[b][:], grouped[b][:].rearrange("p z c t -> p (z c t)"))
+
+        for b in range(2):
+            interleave(b, 0)
+
+        g_banks, part_b = [], []
+        for b in range(BLOCKS):
+            cols = slice(b * P, (b + 1) * P)
+            zb_bank = psum.tile([P, SLOTS], F32, name=f"z{b}")
+            nc.tensor.matmul_mx(zb_bank[:], lhsT=wb[:, cols].bitcast(FP8X4), lhsT_scale=planes[:, 1, cols],
+                                rhs=xb[:].bitcast(FP4X4), rhs_scale=planes[:, 0, :], start=True, stop=True)
+            g_bank = psum.tile([P, T], F32, name=f"g{b}")
+            nc.tensor.matmul_mx(g_bank[:], lhsT=wg[:, cols].bitcast(FP8X4), lhsT_scale=planes[:, 3, cols],
+                                rhs=xg[:].bitcast(FP4X4), rhs_scale=planes[:, 2, :], start=True, stop=True)
+            g_banks.append(g_bank)
+            zb = tile(f"zb{b}", [P, SLOTS], F32)
+            if b == 0:
+                nc.vector.tensor_copy(zb[:], zb_bank[:])
+            else:
+                nc.scalar.copy(zb[:], zb_bank[:])
+            rest = tile(f"rest{b}", [P, T], F32)
+            nc.scalar.activation(rest[:], g_bank[:], SIGMOID, scale=-1.0)
+            pb = tile(f"pb{b}", [P, T], F32)
+            for h in range(2):
+                gated(pb, zb, list_b, rest, h)
+            part_b.append(pb)
+            if b == 1:
+                interleave(0, 1)
+                interleave(1, 1)
+            if b >= 2:
+                quantize(b - 2)
+
+        gates, zas = {}, {}
+
+        def product_a(b):
+            za_bank = psum.tile([P, SLOTS], F32, name=f"z{b}")
+            for z in range(PASSES):
+                cols = slice(z * P, (z + 1) * P)
+                nc.tensor.matmul_mx(za_bank[:], lhsT=codes[b][:, cols].bitcast(FP8X4), lhsT_scale=wa_planes[b][:, cols],
+                                    rhs=xa[:, z, :].bitcast(FP8X4), rhs_scale=planes[:, 4 + z, :],
+                                    start=(z == 0), stop=(z == PASSES - 1))
+            gates[b] = tile(f"gate{b}", [P, T], F32)
+            nc.scalar.activation(gates[b][:], g_banks[b][:], SIGMOID)
+            zas[b] = tile(f"za{b}", [P, SLOTS], F32)
+            nc.scalar.copy(zas[b][:], za_bank[:])
+
+        def combine(b):
+            pa = tile(f"pa{b}", [P, T], F32)
+            y = tile(f"y{b}", [P, T], F32)
+            for h in range(2):
+                gated(pa, zas[b], list_a, gates[b], h)
+            for h in range(2):
+                cols = slice(h * HALF, (h + 1) * HALF)
+                nc.vector.tensor_tensor(y[:, cols], pa[:, cols], part_b[b][:, cols], ADD)
+                nc.sync.dma_start(out[b * P:(b + 1) * P, cols], y[:, cols])
+
+        product_a(0)
+        product_a(1)
+        for b in range(BLOCKS):
+            if b < 2:
+                interleave(b + 2, 0)
+                interleave(b + 2, 1)
+            combine(b)
+            if b < 2:
+                quantize(b + 2)
+                product_a(b + 2)

@@ -21,6 +21,7 @@ PACK = 4
 PASSES = 2
 BLOCKS = N // P
 HALF = T // 2
+SPARE = 32
 
 
 def tile_moe_combine_gated_by_token_kernel(
@@ -35,69 +36,87 @@ def tile_moe_combine_gated_by_token_kernel(
         def tile(name, shape, dtype):
             return held.tile(shape, dtype, name=name, align_bytes=64)
 
-        late = ctx.enter_context(tc.tile_pool(name="late", bufs=1))
-        stage = late.tile([P, 6, 4, 128], I32, name="stage", offset=2048)
-        planes = tile("planes", [P, 6, 512], U8)
+        stage = tile("stage", [P, 4, 4, 128], I32)
+        planes = tile("planes", [P, 4, 512], U8)
+        xa_plane = tile("xa_plane", [P, PASSES, 512], U8)
         nc.vector.memset(planes[:].bitcast(I32), 0)
-        for j, scales in ((0, xb_scales), (1, wb_scales), (2, xg_scales), (3, wg_scales), (4, xa_scales)):
-            passes = scales.shape[0]
-            nc.sync.dma_start(
-                stage[0:4, j:j + passes].rearrange("r z q c -> r (z q) c"),
-                scales.rearrange("z (q r) c -> r (z q) c", r=4).bitcast(I32),
-            )
+        nc.vector.memset(xa_plane[:].bitcast(I32), 0)
+        zbs = [tile(f"zb{b}", [P, SLOTS + SPARE], F32) for b in range(BLOCKS)]
+        zas = [tile(f"za{b}", [P, SLOTS + SPARE], F32) for b in range(BLOCKS)]
+        for table in zbs + zas:
+            nc.gpsimd.memset(table[:, SLOTS:], 0.0)
+        for j, scales in enumerate((xb_scales, wb_scales, xg_scales, wg_scales)):
+            nc.sync.dma_start(stage[0:4, j], scales[0].rearrange("(q r) c -> r q c", r=4).bitcast(I32))
 
-        def load_wa(dst, h, z):
-            nc.sync.dma_start(dst[:], wa[512 * z:512 * (z + 1), 256 * h:256 * (h + 1)].rearrange("(p j) c -> p j c", j=PACK))
+        raw = {(h, z): tile(f"raw{h}{z}", [P, PACK, 256], F32) for h in range(2) for z in range(PASSES)}
+
+        def load_wa(h, z):
+            nc.sync.dma_start(raw[h, z][:], wa[512 * z:512 * (z + 1), 256 * h:256 * (h + 1)].rearrange("(p j) c -> p j c", j=PACK))
+
+        def load_xa_scales(r):
+            nc.sync.dma_start(
+                xa_plane[r:P:32, :, :].bitcast(I32),
+                xa_scales.rearrange("z (q r) c -> r q z c", r=4)[r].bitcast(I32),
+            )
 
         xb = tile("xb", [P, 2 * SLOTS], U8)
         wb = tile("wb", [P, N], I32)
         xg = tile("xg", [P, 2 * T], U8)
         wg = tile("wg", [P, N], I32)
+        xa = tile("xa", [P, PASSES, SLOTS], I32)
         list_a = held.tile([P, T // 16], U16, name="list_a")
         list_b = held.tile([P, T // 16], U16, name="list_b")
-        raw = {(0, 0): tile("raw00", [P, PACK, 256], F32)}
-        nc.sync.dma_start(xb[:].bitcast(I32), xb_words[0].bitcast(I32))
-        nc.sync.dma_start(wb[:], wb_words[0].rearrange("p n t -> p (n t)").bitcast(I32))
-        load_wa(raw[0, 0], 0, 0)
-        nc.sync.dma_start(wg[:], wg_words[0].rearrange("p n t -> p (n t)").bitcast(I32))
-        nc.sync.dma_start(xg[:].bitcast(I32), xg_words[0].bitcast(I32))
+        def load_xb():
+            nc.sync.dma_start(xb[:].bitcast(I32), xb_words[0].bitcast(I32))
+        def load_xg():
+            nc.sync.dma_start(xg[:].bitcast(I32), xg_words[0].bitcast(I32))
+        def load_wb():
+            nc.sync.dma_start(wb[:], wb_words[0].rearrange("p n t -> p (n t)").bitcast(I32))
+        def load_wg():
+            nc.sync.dma_start(wg[:], wg_words[0].rearrange("p n t -> p (n t)").bitcast(I32))
+        def load_xa():
+            nc.sync.dma_start(xa[:], xa_words.rearrange("z p c t -> p z (c t)").bitcast(I32))
+        def spread():
+            words = planes[:].bitcast(I32)
+            nc.vector.tensor_copy(words[0:4], stage[0:4, :, 0])
+            for q in range(1, 4):
+                nc.scalar.dma_start(words[32 * q:32 * q + 4], stage[0:4, :, q])
+        load_xb()
+        load_xg()
+        load_wb()
+        load_wg()
+        spread()
         nc.sync.dma_start(list_b[:], offs2)
         nc.sync.dma_start(list_a[:], offs)
+        load_xa_scales(0)
+        load_wa(0, 0)
+        load_wa(0, 1)
+        load_xa()
+        load_xa_scales(1)
+        load_xa_scales(2)
+        load_xa_scales(3)
+        load_wa(1, 0)
+        load_wa(1, 1)
 
-        words = planes[:].bitcast(I32)
-        nc.vector.tensor_copy(words[0:4], stage[0:4, :, 0])
-        for q in range(1, 4):
-            nc.scalar.dma_start(words[32 * q:32 * q + 4], stage[0:4, :, q])
+        def gated(dst, table, lst, gate, lo, hi):
+            nc.vector.tensor_tensor(dst[:, lo:hi], table[:].indirect(lst[:, lo // 16:hi // 16]), gate[:, lo:hi], MULT)
 
-        raw[0, 1] = late.tile([P, PACK, 256], F32, name="raw01", offset=0)
-        load_wa(raw[0, 1], 0, 1)
-        xa = late.tile([P, PASSES, SLOTS], I32, name="xa", offset=4096, align_bytes=64)
-        nc.sync.dma_start(xa[:], xa_words.rearrange("z p c t -> p z (c t)").bitcast(I32))
-        for z in range(PASSES):
-            raw[1, z] = late.tile([P, PACK, 256], F32, name=f"raw1{z}", offset=4096 * (z + 2))
-            load_wa(raw[1, z], 1, z)
+        codes = [tile(f"code{h}", [P, PASSES, 2 * P], I32) for h in range(2)]
+        wa_planes = [tile(f"wa_plane{h}", [P, PASSES, 2 * P], U8) for h in range(2)]
+        grouped = {}
 
-        def gated(dst, table, lst, gate, h):
-            cols = slice(h * HALF, (h + 1) * HALF)
-            nc.vector.tensor_tensor(dst[:, cols], table[:].indirect(lst[:, h * 16:(h + 1) * 16]), gate[:, cols], MULT)
-
-        grouped = [tile(f"grouped{b}", [P, PASSES, P, PACK], BF16) for b in range(BLOCKS)]
-        codes = [tile(f"code{b}", [P, PASSES * P], I32) for b in range(BLOCKS)]
-        wa_planes = [tile(f"wa_plane{b}", [P, PASSES * P], U8) for b in range(BLOCKS)]
-
-        def interleave(b, z):
-            src = raw[b // 2, z][:, :, (b % 2) * P:(b % 2 + 1) * P].rearrange("p t (c i) -> p c t i", i=4)
-            dst = grouped[b][:, z].rearrange("p (c i) t -> p c t i", i=4)
-            if b < 2:
-                nc.vector.tensor_copy(dst, src)
-            else:
+        def interleave(h, z):
+            if z == 0:
+                grouped[h] = tile("grouped0" if h == 0 else "wg", [P, PASSES, 2 * P, PACK], BF16)
+            src = raw[h, z][:].rearrange("p t (c i) -> p c t i", i=4)
+            dst = grouped[h][:, z].rearrange("p (c i) t -> p c t i", i=4)
+            if h == 1:
                 nc.scalar.copy(dst, src)
+            else:
+                nc.vector.tensor_copy(dst, src)
 
-        def quantize(b):
-            nc.vector.quantize_mx(codes[b][:].bitcast(FP8X4), wa_planes[b][:], grouped[b][:].rearrange("p z c t -> p (z c t)"))
-
-        for b in range(2):
-            interleave(b, 0)
+        def quantize(h):
+            nc.vector.quantize_mx(codes[h][:].rearrange("p z c -> p (z c)").bitcast(FP8X4), wa_planes[h][:].rearrange("p z c -> p (z c)"), grouped[h][:].rearrange("p z c t -> p (z c t)"))
 
         g_banks, part_b = [], []
         for b in range(BLOCKS):
@@ -109,54 +128,56 @@ def tile_moe_combine_gated_by_token_kernel(
             nc.tensor.matmul_mx(g_bank[:], lhsT=wg[:, cols].bitcast(FP8X4), lhsT_scale=planes[:, 3, cols],
                                 rhs=xg[:].bitcast(FP4X4), rhs_scale=planes[:, 2, :], start=True, stop=True)
             g_banks.append(g_bank)
-            zb = tile(f"zb{b}", [P, SLOTS], F32)
             if b == 0:
-                nc.vector.tensor_copy(zb[:], zb_bank[:])
+                nc.vector.tensor_copy(zbs[b][:, :SLOTS], zb_bank[:])
             else:
-                nc.scalar.copy(zb[:], zb_bank[:])
+                nc.scalar.copy(zbs[b][:, :SLOTS], zb_bank[:])
             rest = tile(f"rest{b}", [P, T], F32)
             nc.scalar.activation(rest[:], g_bank[:], SIGMOID, scale=-1.0)
             pb = tile(f"pb{b}", [P, T], F32)
-            for h in range(2):
-                gated(pb, zb, list_b, rest, h)
+            gated(pb, zbs[b], list_b, rest, 0, T)
             part_b.append(pb)
-            if b == 1:
-                interleave(0, 1)
-                interleave(1, 1)
-            if b >= 2:
-                quantize(b - 2)
+            if b < 2:
+                interleave(0, b)
+            if b == 2:
+                quantize(0)
 
-        gates, zas = {}, {}
+        gates = {}
 
         def product_a(b):
             za_bank = psum.tile([P, SLOTS], F32, name=f"z{b}")
+            cols = slice((b % 2) * P, (b % 2 + 1) * P)
             for z in range(PASSES):
-                cols = slice(z * P, (z + 1) * P)
-                nc.tensor.matmul_mx(za_bank[:], lhsT=codes[b][:, cols].bitcast(FP8X4), lhsT_scale=wa_planes[b][:, cols],
-                                    rhs=xa[:, z, :].bitcast(FP8X4), rhs_scale=planes[:, 4 + z, :],
+                nc.tensor.matmul_mx(za_bank[:], lhsT=codes[b // 2][:, z, cols].bitcast(FP8X4), lhsT_scale=wa_planes[b // 2][:, z, cols],
+                                    rhs=xa[:, z, :].bitcast(FP8X4), rhs_scale=xa_plane[:, z, :],
                                     start=(z == 0), stop=(z == PASSES - 1))
-            gates[b] = tile(f"gate{b}", [P, T], F32)
-            nc.scalar.activation(gates[b][:], g_banks[b][:], SIGMOID)
-            zas[b] = tile(f"za{b}", [P, SLOTS], F32)
-            nc.scalar.copy(zas[b][:], za_bank[:])
+            if b == 0:
+                gates[0] = tile("wb", [P, T], F32)[:]
+            if b == 1:
+                later = tile("raw11", [P, BLOCKS - 1, T], F32)
+                for c in range(1, BLOCKS):
+                    gates[c] = later[:, c - 1]
+            nc.scalar.activation(gates[b], g_banks[b][:], SIGMOID)
+            nc.scalar.copy(zas[b][:, :SLOTS], za_bank[:])
 
         def combine(b):
-            pa = tile(f"pa{b}", [P, T], F32)
+            pa = tile("wg" if b == 1 else f"pa{b}", [P, T], F32)
             y = tile(f"y{b}", [P, T], F32)
-            for h in range(2):
-                gated(pa, zas[b], list_a, gates[b], h)
-            for h in range(2):
-                cols = slice(h * HALF, (h + 1) * HALF)
-                nc.vector.tensor_tensor(y[:, cols], pa[:, cols], part_b[b][:, cols], ADD)
-                nc.sync.dma_start(out[b * P:(b + 1) * P, cols], y[:, cols])
+            pieces = [(0, T)] if b < BLOCKS - 1 else [(0, HALF), (HALF, T)]
+            for lo, hi in pieces:
+                gated(pa, zas[b], list_a, gates[b], lo, hi)
+            for lo, hi in pieces:
+                nc.vector.tensor_tensor(y[:, lo:hi], pa[:, lo:hi], part_b[b][:, lo:hi], ADD)
+                nc.sync.dma_start(out[b * P:(b + 1) * P, lo:hi], y[:, lo:hi])
 
+        interleave(1, 0)
         product_a(0)
+        interleave(1, 1)
+        combine(0)
+        quantize(1)
         product_a(1)
-        for b in range(BLOCKS):
-            if b < 2:
-                interleave(b + 2, 0)
-                interleave(b + 2, 1)
-            combine(b)
-            if b < 2:
-                quantize(b + 2)
-                product_a(b + 2)
+        combine(1)
+        product_a(2)
+        combine(2)
+        product_a(3)
+        combine(3)

@@ -42,8 +42,8 @@ def tile_moe_combine_gated_by_token_kernel(
         nc.vector.memset(planes[:].bitcast(I32), 0)
         nc.vector.memset(xa_plane[:].bitcast(I32), 0)
         zbs = [tile(f"zb{b}", [P, SLOTS + SPARE], F32) for b in range(BLOCKS)]
-        zas = [tile(f"za{b}", [P, SLOTS + SPARE], F32) for b in range(BLOCKS)]
-        for table in zbs + zas:
+        zas = {b: tile(f"za{b}", [P, SLOTS + SPARE], F32) for b in range(BLOCKS)}
+        for table in zbs + list(zas.values()):
             nc.gpsimd.memset(table[:, SLOTS:], 0.0)
         for j, scales in enumerate((xb_scales, wb_scales, xg_scales, wg_scales)):
             nc.sync.dma_start(stage[0:4, j], scales[0].rearrange("(q r) c -> r q c", r=4).bitcast(I32))
@@ -101,83 +101,97 @@ def tile_moe_combine_gated_by_token_kernel(
         def gated(dst, table, lst, gate, lo, hi):
             nc.vector.tensor_tensor(dst[:, lo:hi], table[:].indirect(lst[:, lo // 16:hi // 16]), gate[:, lo:hi], MULT)
 
-        codes = [tile(f"code{h}", [P, PASSES, 2 * P], I32) for h in range(2)]
-        wa_planes = [tile(f"wa_plane{h}", [P, PASSES, 2 * P], U8) for h in range(2)]
-        grouped = {}
+        codes, wa_planes, grouped = {}, {}, {}
+        groups = [(0, 0, 2 * P), (1, 0, P), (1, P, 2 * P)]
 
-        def interleave(h, z):
+        def interleave(u, z):
+            h, lo, hi = groups[u]
             if z == 0:
-                grouped[h] = tile("grouped0" if h == 0 else "wg", [P, PASSES, 2 * P, PACK], BF16)
-            src = raw[h, z][:].rearrange("p t (c i) -> p c t i", i=4)
-            dst = grouped[h][:, z].rearrange("p (c i) t -> p c t i", i=4)
-            if h == 1:
-                nc.scalar.copy(dst, src)
-            else:
+                grouped[u] = tile(f"grouped{u}", [P, PASSES, hi - lo, PACK], BF16)
+            src = raw[h, z][:, :, lo:hi].rearrange("p t (c i) -> p c t i", i=4)
+            dst = grouped[u][:, z].rearrange("p (c i) t -> p c t i", i=4)
+            if (u, z) == (0, 0):
                 nc.vector.tensor_copy(dst, src)
+            else:
+                nc.scalar.copy(dst, src)
 
-        def quantize(h):
-            nc.vector.quantize_mx(codes[h][:].rearrange("p z c -> p (z c)").bitcast(FP8X4), wa_planes[h][:].rearrange("p z c -> p (z c)"), grouped[h][:].rearrange("p z c t -> p (z c t)"))
+        def quantize(u):
+            h, lo, hi = groups[u]
+            code = tile(f"code{u}", [P, PASSES, hi - lo], I32)
+            plane = tile(f"wa_plane{u}", [P, PASSES, hi - lo], U8)
+            nc.vector.quantize_mx(code[:].rearrange("p z c -> p (z c)").bitcast(FP8X4), plane[:].rearrange("p z c -> p (z c)"), grouped[u][:].rearrange("p z c t -> p (z c t)"))
+            for c in range(lo, hi, P):
+                codes[2 * h + c // P] = code[:, :, c - lo:c - lo + P]
+                wa_planes[2 * h + c // P] = plane[:, :, c - lo:c - lo + P]
 
         g_banks, part_b = [], []
         for b in range(BLOCKS):
             cols = slice(b * P, (b + 1) * P)
-            zb_bank = psum.tile([P, SLOTS], F32, name=f"z{b}")
+            zb_bank = psum.tile([P, SLOTS], F32, name=f"z{b % 3}")
             nc.tensor.matmul_mx(zb_bank[:], lhsT=wb[:, cols].bitcast(FP8X4), lhsT_scale=planes[:, 1, cols],
                                 rhs=xb[:].bitcast(FP4X4), rhs_scale=planes[:, 0, :], start=True, stop=True)
-            g_bank = psum.tile([P, T], F32, name=f"g{b}")
-            nc.tensor.matmul_mx(g_bank[:], lhsT=wg[:, cols].bitcast(FP8X4), lhsT_scale=planes[:, 3, cols],
-                                rhs=xg[:].bitcast(FP4X4), rhs_scale=planes[:, 2, :], start=True, stop=True)
-            g_banks.append(g_bank)
             if b == 0:
                 nc.vector.tensor_copy(zbs[b][:, :SLOTS], zb_bank[:])
             else:
                 nc.scalar.copy(zbs[b][:, :SLOTS], zb_bank[:])
+            pieces = [(0, T)] if b > 0 else [(0, HALF), (HALF, T)]
             rest = tile(f"rest{b}", [P, T], F32)
-            nc.scalar.activation(rest[:], g_bank[:], SIGMOID, scale=-1.0)
             pb = tile(f"pb{b}", [P, T], F32)
-            gated(pb, zbs[b], list_b, rest, 0, T)
+            g_banks.append([])
+            for lo, hi in pieces:
+                g_bank = psum.tile([P, hi - lo], F32, name=f"g{b}_{lo}")
+                nc.tensor.matmul_mx(g_bank[:], lhsT=wg[:, cols].bitcast(FP8X4), lhsT_scale=planes[:, 3, cols],
+                                    rhs=xg[:, 2 * lo:2 * hi].bitcast(FP4X4), rhs_scale=planes[:, 2, lo:hi], start=True, stop=True)
+                g_banks[b].append((lo, hi, g_bank))
+                nc.scalar.activation(rest[:, lo:hi], g_bank[:], SIGMOID, scale=-1.0)
+                gated(pb, zbs[b], list_b, rest, lo, hi)
             part_b.append(pb)
             if b < 2:
                 interleave(0, b)
-            if b == 2:
+            if b == 1:
                 quantize(0)
+
+        gate_tiles = {}
+
+        def gate(b):
+            if b % 2 == 0:
+                gate_tiles[b // 2] = tile("wb" if b == 0 else "raw10", [P, 2, T], F32)
+            return gate_tiles[b // 2][:, b % 2]
 
         gates = {}
 
         def product_a(b):
-            za_bank = psum.tile([P, SLOTS], F32, name=f"z{b}")
-            cols = slice((b % 2) * P, (b % 2 + 1) * P)
+            za_bank = psum.tile([P, SLOTS], F32, name=f"z{(b + 1) % 3}")
             for z in range(PASSES):
-                nc.tensor.matmul_mx(za_bank[:], lhsT=codes[b // 2][:, z, cols].bitcast(FP8X4), lhsT_scale=wa_planes[b // 2][:, z, cols],
+                nc.tensor.matmul_mx(za_bank[:], lhsT=codes[b][:, z].bitcast(FP8X4), lhsT_scale=wa_planes[b][:, z],
                                     rhs=xa[:, z, :].bitcast(FP8X4), rhs_scale=xa_plane[:, z, :],
                                     start=(z == 0), stop=(z == PASSES - 1))
-            if b == 0:
-                gates[0] = tile("wb", [P, T], F32)[:]
-            if b == 1:
-                later = tile("raw11", [P, BLOCKS - 1, T], F32)
-                for c in range(1, BLOCKS):
-                    gates[c] = later[:, c - 1]
-            nc.scalar.activation(gates[b], g_banks[b][:], SIGMOID)
+            gates[b] = gate(b)
+            for lo, hi, g_bank in g_banks[b]:
+                nc.scalar.activation(gates[b][:, lo:hi], g_bank[:], SIGMOID)
             nc.scalar.copy(zas[b][:, :SLOTS], za_bank[:])
 
-        def combine(b):
-            pa = tile("wg" if b == 1 else f"pa{b}", [P, T], F32)
-            y = tile(f"y{b}", [P, T], F32)
-            pieces = [(0, T)] if b < BLOCKS - 1 else [(0, HALF), (HALF, T)]
+        part_a = [tile(f"pa{b}", [P, T], F32) for b in range(BLOCKS)]
+
+        def add(b, tag, pieces):
+            y = tile(tag, [P, T], F32)
             for lo, hi in pieces:
-                gated(pa, zas[b], list_a, gates[b], lo, hi)
-            for lo, hi in pieces:
-                nc.vector.tensor_tensor(y[:, lo:hi], pa[:, lo:hi], part_b[b][:, lo:hi], ADD)
+                nc.vector.tensor_tensor(y[:, lo:hi], part_a[b][:, lo:hi], part_b[b][:, lo:hi], ADD)
                 nc.sync.dma_start(out[b * P:(b + 1) * P, lo:hi], y[:, lo:hi])
 
-        interleave(1, 0)
-        product_a(0)
-        interleave(1, 1)
-        combine(0)
-        quantize(1)
-        product_a(1)
-        combine(1)
-        product_a(2)
-        combine(2)
-        product_a(3)
-        combine(3)
+        for b in range(BLOCKS - 1):
+            product_a(b)
+            if b < 2:
+                interleave(b + 1, 0)
+                interleave(b + 1, 1)
+            gated(part_a[b], zas[b], list_a, gates[b], 0, T)
+            if b < 2:
+                quantize(b + 1)
+            if b > 0:
+                add(b - 1, f"za{b}", [(0, T)])
+        last = BLOCKS - 1
+        product_a(last)
+        gated(part_a[last], zas[last], list_a, gates[last], 0, HALF)
+        add(last - 1, "y2", [(0, T)])
+        gated(part_a[last], zas[last], list_a, gates[last], HALF, T)
+        add(last, "y3", [(0, HALF), (HALF, T)])

from contextlib import ExitStack

import concourse.mybir as mybir

K, SLOTS, T, N = 1024, 512, 512, 512
FLOPS = 2 * N * (K * SLOTS + 512 * SLOTS + 512 * T)

F32 = mybir.dt.float32
BF16 = mybir.dt.bfloat16
I32 = mybir.dt.int32
U16 = mybir.dt.uint16
U8 = mybir.dt.uint8
FP8X4 = mybir.dt.float8_e4m3fn_x4
FP4X4 = mybir.dt.float4_e2m1fn_x4
SIGMOID = mybir.ActivationFunctionType.Sigmoid
MULT = mybir.AluOpType.mult
ADD = mybir.AluOpType.add

P = 128
PACK = 4
PASSES = 2
BLOCKS = N // P
HALF = T // 2
SPARE = 32


def tile_moe_combine_gated_by_token_kernel(
    tc, xa_words, xa_scales, wa, xb_words, xb_scales, wb_words, wb_scales,
    xg_words, xg_scales, wg_words, wg_scales, offs, offs2, out,
):
    nc = tc.nc
    with ExitStack() as ctx:
        held = ctx.enter_context(tc.tile_pool(name="held", bufs=1))
        psum = ctx.enter_context(tc.psum_pool(name="psum", bufs=1))

        def tile(name, shape, dtype):
            return held.tile(shape, dtype, name=name, align_bytes=64)

        stage = tile("stage", [P, 4, 4, 128], I32)
        planes = tile("planes", [P, 4, 512], U8)
        xa_plane = tile("xa_plane", [P, PASSES, 512], U8)
        nc.vector.memset(planes[:].bitcast(I32), 0)
        nc.vector.memset(xa_plane[:].bitcast(I32), 0)
        zbs = [tile(f"zb{b}", [P, SLOTS + SPARE], F32) for b in range(BLOCKS)]
        zas = {b: tile(f"za{b}", [P, SLOTS + SPARE], F32) for b in range(BLOCKS)}
        for table in zbs + list(zas.values()):
            nc.gpsimd.memset(table[:, SLOTS:], 0.0)
        for j, scales in enumerate((xb_scales, wb_scales, xg_scales, wg_scales)):
            nc.sync.dma_start(stage[0:4, j], scales[0].rearrange("(q r) c -> r q c", r=4).bitcast(I32))

        raw = {(h, z): tile(f"raw{h}{z}", [P, PACK, 256], F32) for h in range(2) for z in range(PASSES)}

        def load_wa(h, z):
            nc.sync.dma_start(raw[h, z][:], wa[512 * z:512 * (z + 1), 256 * h:256 * (h + 1)].rearrange("(p j) c -> p j c", j=PACK))

        def load_xa_scales(r):
            nc.sync.dma_start(
                xa_plane[r:P:32, :, :].bitcast(I32),
                xa_scales.rearrange("z (q r) c -> r q z c", r=4)[r].bitcast(I32),
            )

        xb = tile("xb", [P, 2 * SLOTS], U8)
        wb = tile("wb", [P, N], I32)
        xg = tile("xg", [P, 2 * T], U8)
        wg = tile("wg", [P, N], I32)
        xa = tile("xa", [P, PASSES, SLOTS], I32)
        list_a = held.tile([P, T // 16], U16, name="list_a")
        list_b = held.tile([P, T // 16], U16, name="list_b")
        def load_xb():
            nc.sync.dma_start(xb[:].bitcast(I32), xb_words[0].bitcast(I32))
        def load_xg():
            nc.sync.dma_start(xg[:].bitcast(I32), xg_words[0].bitcast(I32))
        def load_wb():
            nc.sync.dma_start(wb[:], wb_words[0].rearrange("p n t -> p (n t)").bitcast(I32))
        def load_wg():
            nc.sync.dma_start(wg[:], wg_words[0].rearrange("p n t -> p (n t)").bitcast(I32))
        def load_xa():
            nc.sync.dma_start(xa[:], xa_words.rearrange("z p c t -> p z (c t)").bitcast(I32))
        def spread():
            words = planes[:].bitcast(I32)
            nc.vector.tensor_copy(words[0:4], stage[0:4, :, 0])
            for q in range(1, 4):
                nc.scalar.dma_start(words[32 * q:32 * q + 4], stage[0:4, :, q])
        load_xb()
        load_xg()
        load_wb()
        load_wg()
        spread()
        nc.sync.dma_start(list_b[:], offs2)
        nc.sync.dma_start(list_a[:], offs)
        load_xa_scales(0)
        load_wa(0, 0)
        load_wa(0, 1)
        load_xa()
        load_xa_scales(1)
        load_xa_scales(2)
        load_xa_scales(3)
        load_wa(1, 0)
        load_wa(1, 1)

        def gated(dst, table, lst, gate, lo, hi):
            nc.vector.tensor_tensor(dst[:, lo:hi], table[:].indirect(lst[:, lo // 16:hi // 16]), gate[:, lo:hi], MULT)

        codes, wa_planes, grouped = {}, {}, {}
        groups = [(0, 0, 2 * P), (1, 0, P), (1, P, 2 * P)]

        def interleave(u, z):
            h, lo, hi = groups[u]
            if z == 0:
                grouped[u] = tile(f"grouped{u}", [P, PASSES, hi - lo, PACK], BF16)
            src = raw[h, z][:, :, lo:hi].rearrange("p t (c i) -> p c t i", i=4)
            dst = grouped[u][:, z].rearrange("p (c i) t -> p c t i", i=4)
            if (u, z) == (0, 0):
                nc.vector.tensor_copy(dst, src)
            else:
                nc.scalar.copy(dst, src)

        def quantize(u):
            h, lo, hi = groups[u]
            code = tile(f"code{u}", [P, PASSES, hi - lo], I32)
            plane = tile(f"wa_plane{u}", [P, PASSES, hi - lo], U8)
            nc.vector.quantize_mx(code[:].rearrange("p z c -> p (z c)").bitcast(FP8X4), plane[:].rearrange("p z c -> p (z c)"), grouped[u][:].rearrange("p z c t -> p (z c t)"))
            for c in range(lo, hi, P):
                codes[2 * h + c // P] = code[:, :, c - lo:c - lo + P]
                wa_planes[2 * h + c // P] = plane[:, :, c - lo:c - lo + P]

        g_banks, part_b = [], []
        for b in range(BLOCKS):
            cols = slice(b * P, (b + 1) * P)
            zb_bank = psum.tile([P, SLOTS], F32, name=f"z{b % 3}")
            nc.tensor.matmul_mx(zb_bank[:], lhsT=wb[:, cols].bitcast(FP8X4), lhsT_scale=planes[:, 1, cols],
                                rhs=xb[:].bitcast(FP4X4), rhs_scale=planes[:, 0, :], start=True, stop=True)
            if b == 0:
                nc.vector.tensor_copy(zbs[b][:, :SLOTS], zb_bank[:])
            else:
                nc.scalar.copy(zbs[b][:, :SLOTS], zb_bank[:])
            pieces = [(0, T)] if b > 0 else [(0, HALF), (HALF, T)]
            rest = tile(f"rest{b}", [P, T], F32)
            pb = tile(f"pb{b}", [P, T], F32)
            g_banks.append([])
            for lo, hi in pieces:
                g_bank = psum.tile([P, hi - lo], F32, name=f"g{b}_{lo}")
                nc.tensor.matmul_mx(g_bank[:], lhsT=wg[:, cols].bitcast(FP8X4), lhsT_scale=planes[:, 3, cols],
                                    rhs=xg[:, 2 * lo:2 * hi].bitcast(FP4X4), rhs_scale=planes[:, 2, lo:hi], start=True, stop=True)
                g_banks[b].append((lo, hi, g_bank))
                nc.scalar.activation(rest[:, lo:hi], g_bank[:], SIGMOID, scale=-1.0)
                gated(pb, zbs[b], list_b, rest, lo, hi)
            part_b.append(pb)
            if b < 2:
                interleave(0, b)
            if b == 1:
                quantize(0)

        gate_tiles = {}

        def gate(b):
            if b % 2 == 0:
                gate_tiles[b // 2] = tile("wb" if b == 0 else "raw10", [P, 2, T], F32)
            return gate_tiles[b // 2][:, b % 2]

        gates = {}

        def product_a(b):
            za_bank = psum.tile([P, SLOTS], F32, name=f"z{(b + 1) % 3}")
            for z in range(PASSES):
                nc.tensor.matmul_mx(za_bank[:], lhsT=codes[b][:, z].bitcast(FP8X4), lhsT_scale=wa_planes[b][:, z],
                                    rhs=xa[:, z, :].bitcast(FP8X4), rhs_scale=xa_plane[:, z, :],
                                    start=(z == 0), stop=(z == PASSES - 1))
            gates[b] = gate(b)
            for lo, hi, g_bank in g_banks[b]:
                nc.scalar.activation(gates[b][:, lo:hi], g_bank[:], SIGMOID)
            nc.scalar.copy(zas[b][:, :SLOTS], za_bank[:])

        part_a = [tile(f"pa{b}", [P, T], F32) for b in range(BLOCKS)]

        def add(b, tag, pieces):
            y = tile(tag, [P, T], F32)
            for lo, hi in pieces:
                nc.vector.tensor_tensor(y[:, lo:hi], part_a[b][:, lo:hi], part_b[b][:, lo:hi], ADD)
                nc.sync.dma_start(out[b * P:(b + 1) * P, lo:hi], y[:, lo:hi])

        for b in range(BLOCKS - 1):
            product_a(b)
            if b < 2:
                interleave(b + 1, 0)
                interleave(b + 1, 1)
            gated(part_a[b], zas[b], list_a, gates[b], 0, T)
            if b < 2:
                quantize(b + 1)
            if b > 0:
                add(b - 1, f"za{b}", [(0, T)])
        last = BLOCKS - 1
        product_a(last)
        gated(part_a[last], zas[last], list_a, gates[last], 0, HALF)
        add(last - 1, "y2", [(0, T)])
        gated(part_a[last], zas[last], list_a, gates[last], HALF, T)
        add(last, "y3", [(0, HALF), (HALF, T)])
